import numpy as np
import ml_dtypes


def mxq(x, axis, fmt="e4m3"):
    dtype, down = {"e4m3": (ml_dtypes.float8_e4m3fn, 7), "e5m2": (ml_dtypes.float8_e5m2, 14)}[fmt]
    v = np.moveaxis(np.asarray(x, np.float32).astype(ml_dtypes.bfloat16).astype(np.float64), axis, -1)
    blocks = v.reshape(v.shape[:-1] + (-1, 32))
    amax = np.abs(blocks).max(-1, keepdims=True)
    byte = np.maximum(np.where(amax > 0, np.frexp(amax)[1] - 1 + 127, 0) - down, 1)
    scale = np.exp2(byte - 127.0)
    codes = (blocks / scale).astype(np.float32).astype(dtype).astype(np.float64)
    return np.moveaxis((codes * scale).reshape(v.shape), -1, axis)


WIDE = False


def mx_kscale(k):
    if not WIDE:
        return np.ones(k)
    levels = np.array([30, -30])
    if k % 512:
        return np.exp2(np.random.permutation(np.resize(levels, k // 32))).repeat(32)
    a = np.empty((k // 512, 16))
    for p in range(k // 512):
        a[p, :8] = np.random.permutation(np.resize(levels, 8))
        for g in range(8):
            far = levels[np.abs(levels - a[p, g]) >= 10]
            a[p, g + 8] = far[np.random.randint(len(far))]
    return np.exp2(a.ravel()).repeat(32)


def f64(x):
    return np.asarray(x).astype(np.float64)


def striped(idx):
    return np.tile(np.asarray(idx).reshape(-1, 16).T, (8, 1)).astype(np.uint16)


def unstriped(offs):
    return offs[:16].T.reshape(-1).astype(np.int64)


E2M1 = np.array([0.0, 0.5, 1.0, 1.5, 2.0, 3.0, 4.0, 6.0, -0.0, -0.5, -1.0, -1.5, -2.0, -3.0, -4.0, -6.0])


def pack_weight(w, fmt):
    k, n = w.shape
    w = f64(np.asarray(w, np.float32).astype(ml_dtypes.bfloat16)).reshape(k // 32, 32, n)
    amax = np.abs(w).max(1)
    if fmt in ("e4m3", "e5m2"):
        byte = np.frexp(amax)[1] - 1 + 127 - (7 if fmt == "e4m3" else 14)
    else:
        mant, ex = np.frexp(amax / 6.0)
        byte = np.where(mant > 0.5, ex, ex - 1) + 127
    byte = np.clip(np.where(amax > 0, byte, 1), 1, 254)
    scaled = (w * np.exp2(127.0 - byte)[:, None, :]).reshape(k, n).astype(np.float32)
    by_word = np.ascontiguousarray(scaled.reshape(k // 512, 128, 4, n).transpose(0, 1, 3, 2))
    if fmt in ("e4m3", "e5m2"):
        words = by_word.astype(ml_dtypes.float8_e4m3fn if fmt == "e4m3" else ml_dtypes.float8_e5m2).view(np.uint8)
    else:
        c = by_word.astype(ml_dtypes.float4_e2m1fn).view(np.uint8) & 0xF
        words = (c[..., 0::2] | (c[..., 1::2] << 4)).reshape(k // 512, 128, 2 * n)
    return np.ascontiguousarray(words), np.ascontiguousarray(byte.astype(np.uint8).reshape(k // 512, 16, n))


def unpack_weight(words, scales, fmt):
    g, _, n = scales.shape
    words = np.ascontiguousarray(words).reshape(g, 128, n, -1)
    if fmt in ("e4m3", "e5m2"):
        vals = words.view(ml_dtypes.float8_e4m3fn if fmt == "e4m3" else ml_dtypes.float8_e5m2).astype(np.float64)
    else:
        nib = np.empty((g, 128, n, 4), np.uint8)
        nib[..., 0::2] = words & 0xF
        nib[..., 1::2] = words >> 4
        vals = E2M1[nib]
    vals = vals * np.repeat(np.exp2(scales.astype(np.float64) - 127.0), 8, axis=1)[..., None]
    return vals.transpose(0, 1, 3, 2).reshape(g * 512, n)


K, T, Z, J, R, N, S = 512, 1024, 1024, 256, 512, 256, 1024


def setup_inputs():
    n = np.random.standard_normal
    idx = np.random.permutation(T)[:J]
    idx2 = np.random.permutation(Z)[:J]
    idx3 = np.random.permutation(J)[:J]
    idx4 = np.random.permutation(J)[:J]
    idx5 = np.random.permutation(S)[:N]
    fk = mx_kscale(K)
    fr = mx_kscale(R)
    xtp = pack_weight(n((K, T)) / fk[:, None], "e2m1")
    xop = pack_weight(n((K, Z)) / fk[:, None], "e5m2")
    wp = pack_weight(n((K, R)) * 1 / np.sqrt(K) * fk[:, None] * fr, "e5m2")
    vsp = pack_weight(n((R, S)) * 1 / np.sqrt(R) / fr[:, None], "e4m3")
    return {
        "xt_words": xtp[0],
        "xt_scales": xtp[1],
        "xo_words": xop[0],
        "xo_scales": xop[1],
        "w_words": wp[0],
        "w_scales": wp[1],
        "vs_words": vsp[0],
        "vs_scales": vsp[1],
        "offs": striped(idx),
        "offs2": striped(idx2),
        "offs3": striped(idx3),
        "offs4": striped(idx4),
        "offs5": striped(idx5),
    }


def reference(xt_words, xt_scales, xo_words, xo_scales, w_words, w_scales, vs_words, vs_scales, offs, offs2, offs3, offs4, offs5):
    idx = unstriped(offs)
    idx2 = unstriped(offs2)
    idx3 = unstriped(offs3)
    idx4 = unstriped(offs4)
    idx5 = unstriped(offs5)
    xtu = unpack_weight(xt_words, xt_scales, "e2m1")
    xou = unpack_weight(xo_words, xo_scales, "e5m2")
    wu = unpack_weight(w_words, w_scales, "e5m2")
    vsu = unpack_weight(vs_words, vs_scales, "e4m3")
    xtidxg = xtu[:, idx]
    a = wu.T @ xtidxg
    xoidx2g = xou[:, idx2]
    b = wu.T @ xoidx2g
    h1 = np.maximum(a, b[:, idx3])
    hid = np.abs(b - h1[:, idx4])
    vsidx5g = vsu[:, idx5]
    hidq = mxq(hid, 0, "e5m2")
    y = vsidx5g.T @ hidq
    return y

from contextlib import ExitStack

import concourse.mybir as mybir

K, T, Z, J, R, N, S = 512, 1024, 1024, 256, 512, 256, 1024
FLOPS = 2 * K * R * J * 2 + 2 * R * N * J

F32 = mybir.dt.float32
BF16 = mybir.dt.bfloat16
I32 = mybir.dt.int32
U32 = mybir.dt.uint32
U16 = mybir.dt.uint16
U8 = mybir.dt.uint8
E4M3 = mybir.dt.float8_e4m3fn_x4
E5M2 = mybir.dt.float8_e5m2_x4
E2M1 = mybir.dt.float4_e2m1fn_x4
ACT = mybir.ActivationFunctionType
ALU = mybir.AluOpType

P = 128
PACK = 4
HALF = J // 2
SPARE = 8


def tile_list_tworounds_oneforboth_store_plain_kernel(
    tc, xt_words, xt_scales, xo_words, xo_scales, w_words, w_scales, vs_words, vs_scales, offs, offs2, offs3, offs4, offs5, out
):
    nc = tc.nc
    with ExitStack() as ctx:
        sb = ctx.enter_context(tc.tile_pool(name="sb", bufs=1))
        ps = ctx.enter_context(tc.psum_pool(name="ps", bufs=1))

        def list_tile(name):
            return sb.tile([P, J // 16], U16, name=name)

        def load_scale_rows(queue, plane, rows):
            for q in range(4):
                queue.dma_start(out=plane[32 * q : 32 * q + 4, :].bitcast(I32), in_=rows[0, 4 * q : 4 * q + 4, :].bitcast(I32))

        def load_scale_rows_repeated(queue, plane, rows):
            words = rows.shape[2] // 4
            for q in range(4):
                four = rows[0, 4 * q : 4 * q + 4, :].bitcast(I32)
                queue.dma_start(out=plane[32 * q : 32 * q + 32, :].bitcast(I32), in_=four.unsqueeze(0).to_broadcast([8, 4, words]))

        def words_view(words):
            return words[0].rearrange("p n t -> p (n t)").bitcast(I32)

        l_xt, l_xo, l_b, l_h, l_vs = [list_tile("list%d" % i) for i in range(5)]
        w_sc = sb.tile([P, R], U8, name="w_sc", align_bytes=64)
        xo_sc = sb.tile([P, Z], U8, name="xo_sc", align_bytes=64)
        xt_sc = sb.tile([P, T], U8, name="xt_sc", align_bytes=64)
        vs_sc = sb.tile([P, S], U8, name="vs_sc", align_bytes=64)
        w_wd = sb.tile([P, R], U32, name="w_wd", align_bytes=64)
        xo_wd = sb.tile([P, Z], U32, name="xo_wd", align_bytes=64)
        xt_wd = sb.tile([P, T], U16, name="xt_wd", align_bytes=64)
        vs_wd = sb.tile([P, S], U32, name="vs_wd", align_bytes=64)
        b_sb = [sb.tile([P, J + SPARE], F32, name="b_sb%d" % t, align_bytes=64) for t in range(PACK)]

        for plane in (xo_sc, xt_sc):
            nc.vector.memset(plane[:].bitcast(I32), 0)
        nc.gpsimd.memset(vs_sc[:].bitcast(I32), 0)
        for t in range(PACK):
            nc.vector.memset(b_sb[t][:, J:], 0.0)

        load_scale_rows_repeated(nc.scalar, w_sc, w_scales)
        nc.sync.dma_start(l_xo[:], offs2)
        nc.sync.dma_start(l_xt[:], offs)
        nc.sync.dma_start(out=w_wd[:].bitcast(I32), in_=words_view(w_words))
        nc.sync.dma_start(out=xo_wd[:].bitcast(I32), in_=words_view(xo_words))
        load_scale_rows(nc.sync, xo_sc, xo_scales)
        nc.sync.dma_start(out=xt_wd[:].bitcast(I32), in_=xt_words[0].bitcast(I32))
        load_scale_rows(nc.sync, xt_sc, xt_scales)
        nc.sync.dma_start(l_b[:], offs3)
        nc.sync.dma_start(out=vs_wd[:].bitcast(I32), in_=words_view(vs_words))
        nc.sync.dma_start(l_vs[:], offs5)
        nc.sync.dma_start(l_h[:], offs4)
        load_scale_rows(nc.gpsimd, vs_sc, vs_scales)

        wp_wd = sb.tile([P, PACK, P], U32, name="wp_wd", align_bytes=64)
        wp_sc = sb.tile([P, PACK, P], U8, name="wp_sc", align_bytes=64)
        nc.vector.tensor_copy(out=wp_sc[:], in_=w_sc[:].rearrange("p (m t) -> p t m", t=PACK))
        nc.vector.tensor_copy(out=wp_wd[:], in_=w_wd[:].rearrange("p (m t) -> p t m", t=PACK))

        def gather_operand(name, words, plane, offsets, dtype):
            g_sc = sb.tile([P, J], U8, name=name + "_gsc", align_bytes=64)
            g_wd = sb.tile([P, J], dtype, name=name + "_gwd", align_bytes=64)
            nc.vector.tensor_copy(out=g_wd[:], in_=words[:].indirect(offsets[:]))
            nc.vector.tensor_copy(out=g_sc[:], in_=plane[:].indirect(offsets[:]))
            return g_wd, g_sc

        xo_g, xo_gs = gather_operand("xo", xo_wd, xo_sc, l_xo, U32)
        b_ps = [ps.tile([P, J], F32, name="b_ps%d" % t) for t in range(PACK)]
        for t in range(PACK):
            nc.tensor.matmul_mx(out=b_ps[t][:], lhsT=wp_wd[:, t, :].bitcast(E5M2), lhsT_scale=wp_sc[:, t, :],
                                rhs=xo_g[:].bitcast(E5M2), rhs_scale=xo_gs[:], start=True, stop=True)
        xt_g, xt_gs = gather_operand("xt", xt_wd, xt_sc, l_xt, U16)
        a_ps = [ps.tile([P, 2, J], F32, name="a_ps%d" % u) for u in range(2)]
        for t in range(PACK):
            nc.tensor.matmul_mx(out=a_ps[t // 2][:, t % 2, :], lhsT=wp_wd[:, t, :].bitcast(E5M2), lhsT_scale=wp_sc[:, t, :],
                                rhs=xt_g[:].bitcast(E2M1), rhs_scale=xt_gs[:], start=True, stop=True)
        vs_g, vs_gs = gather_operand("vs", vs_wd, vs_sc, l_vs, U32)

        bg = [sb.tile([P, J], F32, name="bg%d" % t, align_bytes=64) for t in range(PACK)]
        h1 = [sb.tile([P, J], F32, name="h1_%d" % t, align_bytes=64) for t in range(PACK)]
        diff = [sb.tile([P, PACK, HALF], F32, name="diff%d" % h, align_bytes=64) for h in range(2)]
        hg = [sb.tile([P, HALF], F32, name="hg%d" % t, align_bytes=64) for t in range(PACK)]
        cols = HALF // 16

        def evac_b(t):
            nc.scalar.activation(out=b_sb[t][:, :J], in_=b_ps[t][:], func=ACT.Copy)

        def look_b(t):
            nc.scalar.activation(out=bg[t][:], in_=b_sb[t][:].indirect(l_b[:]), func=ACT.Copy)

        def keep_max(t):
            nc.vector.tensor_tensor(out=h1[t][:], in0=a_ps[t // 2][:, t % 2, :], in1=bg[t][:], op=ALU.max)

        def look_sub(t):
            nc.vector.tensor_tensor(out=diff[0][:, t, :], in0=h1[t][:].indirect(l_h[:, :cols]), in1=b_sb[t][:, :HALF], op=ALU.subtract)

        def look_h(t):
            nc.scalar.activation(out=hg[t][:], in_=h1[t][:].indirect(l_h[:, cols:]), func=ACT.Copy)

        def sub(t):
            nc.vector.tensor_tensor(out=diff[1][:, t, :], in0=hg[t][:], in1=b_sb[t][:, HALF:J], op=ALU.subtract)

        evac_b(0)
        for t in range(PACK):
            if t + 1 < PACK:
                evac_b(t + 1)
            look_b(t)
        keep_max(0)
        for t in range(PACK):
            if t + 1 < PACK:
                keep_max(t + 1)
            look_sub(t)
        for t in range(PACK):
            look_h(t)
        for t in range(PACK):
            sub(t)

        out_v = out.rearrange("(m p) j -> p m j", p=P)
        for h in range(2):
            hid = sb.tile([P, HALF, PACK], BF16, name="hid%d" % h, align_bytes=64)
            nc.scalar.activation(out=hid[:], in_=diff[h][:].rearrange("p t c -> p c t"), func=ACT.Abs)
            q_wd = sb.tile([P, HALF], U32, name="q_wd%d" % h, align_bytes=64)
            q_sc = sb.tile([P, HALF], U8, name="q_sc%d" % h, align_bytes=64)
            nc.vector.quantize_mx(out=q_wd[:].bitcast(E5M2), scales=q_sc[:], in_=hid[:].rearrange("p c t -> p (c t)"))
            o_ps = ps.tile([P, 2, HALF], F32, name="o_ps%d" % h)
            for m in range(2):
                nc.tensor.matmul_mx(out=o_ps[:, m, :], lhsT=vs_g[:, m * P : (m + 1) * P].bitcast(E4M3), lhsT_scale=vs_gs[:, m * P : (m + 1) * P],
                                    rhs=q_wd[:].bitcast(E5M2), rhs_scale=q_sc[:], start=True, stop=True)
            res = sb.tile([P, 2, HALF], F32, name="res%d" % h, align_bytes=64)
            nc.vector.tensor_copy(out=res[:], in_=o_ps[:])
            nc.sync.dma_start(out=out_v[:, :, h * HALF : (h + 1) * HALF], in_=res[:])
